import numpy as np
import ml_dtypes


def mxq(x, axis, fmt="e4m3"):
    dtype, down = {"e4m3": (ml_dtypes.float8_e4m3fn, 7), "e5m2": (ml_dtypes.float8_e5m2, 14)}[fmt]
    v = np.moveaxis(np.asarray(x, np.float32).astype(ml_dtypes.bfloat16).astype(np.float64), axis, -1)
    blocks = v.reshape(v.shape[:-1] + (-1, 32))
    amax = np.abs(blocks).max(-1, keepdims=True)
    byte = np.maximum(np.where(amax > 0, np.frexp(amax)[1] - 1 + 127, 0) - down, 1)
    scale = np.exp2(byte - 127.0)
    codes = (blocks / scale).astype(np.float32).astype(dtype).astype(np.float64)
    return np.moveaxis((codes * scale).reshape(v.shape), -1, axis)


WIDE = False


def mx_kscale(k):
    if not WIDE:
        return np.ones(k)
    levels = np.array([10, -10, 5, -5, 0])
    if k % 512:
        return np.exp2(np.random.permutation(np.resize(levels, k // 32))).repeat(32)
    a = np.empty((k // 512, 16))
    for p in range(k // 512):
        a[p, :8] = np.random.permutation(np.resize(levels, 8))
        for g in range(8):
            far = levels[np.abs(levels - a[p, g]) >= 10]
            a[p, g + 8] = far[np.random.randint(len(far))]
    return np.exp2(a.ravel()).repeat(32)


def f64(x):
    return np.asarray(x).astype(np.float64)


def striped(idx):
    return np.tile(idx.reshape(-1, 16).T, (8, 1)).astype(np.uint16)


def unstriped(offs):
    return offs[:16].T.reshape(-1).astype(np.int64)


E2M1 = np.array([0.0, 0.5, 1.0, 1.5, 2.0, 3.0, 4.0, 6.0, -0.0, -0.5, -1.0, -1.5, -2.0, -3.0, -4.0, -6.0])


def pack_weight(w, fmt):
    k, n = w.shape
    w = f64(np.asarray(w, np.float32).astype(ml_dtypes.bfloat16)).reshape(k // 32, 32, n)
    amax = np.abs(w).max(1)
    if fmt == "e4m3":
        byte = np.frexp(amax)[1] - 1 + 127 - 7
    else:
        mant, ex = np.frexp(amax / 6.0)
        byte = np.where(mant > 0.5, ex, ex - 1) + 127
    byte = np.clip(np.where(amax > 0, byte, 1), 1, 254)
    scaled = (w * np.exp2(127.0 - byte)[:, None, :]).reshape(k, n).astype(np.float32)
    by_word = np.ascontiguousarray(scaled.reshape(k // 512, 128, 4, n).transpose(0, 1, 3, 2))
    if fmt == "e4m3":
        words = by_word.astype(ml_dtypes.float8_e4m3fn).view(np.uint8)
    else:
        c = by_word.astype(ml_dtypes.float4_e2m1fn).view(np.uint8) & 0xF
        words = (c[..., 0::2] | (c[..., 1::2] << 4)).reshape(k // 512, 128, 2 * n)
    return np.ascontiguousarray(words), np.ascontiguousarray(byte.astype(np.uint8).reshape(k // 512, 16, n))


def unpack_weight(words, scales, fmt):
    g, _, n = scales.shape
    words = np.ascontiguousarray(words).reshape(g, 128, n, -1)
    if fmt == "e4m3":
        vals = words.view(ml_dtypes.float8_e4m3fn).astype(np.float64)
    else:
        nib = np.empty((g, 128, n, 4), np.uint8)
        nib[..., 0::2] = words & 0xF
        nib[..., 1::2] = words >> 4
        vals = E2M1[nib]
    vals = vals * np.repeat(np.exp2(scales.astype(np.float64) - 127.0), 8, axis=1)[..., None]
    return vals.transpose(0, 1, 3, 2).reshape(g * 512, n)


K, T, E, C, N = 2560, 640, 8, 128, 128
K8 = 1024


def by_expert(wq, xq):
    return np.concatenate([wq[e].T @ xq[:, e * C:(e + 1) * C] for e in range(E)], axis=1)


def setup_inputs():
    n = np.random.standard_normal
    s = mx_kscale(K)[:, None]
    w = n((E, K, N)) / np.sqrt(K) / s[None]
    w8 = [pack_weight(m[:K8], "e4m3") for m in w]
    w4 = [pack_weight(m[K8:], "e2m1") for m in w]
    idx = np.random.permutation(E * C)
    return {
        "xT": (n((K, T)) * s).astype(np.float32),
        "w8_words": np.stack([m[0] for m in w8]),
        "w8_scales": np.stack([m[1] for m in w8]),
        "w4_words": np.stack([m[0] for m in w4]),
        "w4_scales": np.stack([m[1] for m in w4]),
        "b": (0.3 * n((N, E))).astype(np.float32),
        "gate": np.tile(np.where(idx < T, np.random.uniform(0.2, 1.0, E * C), 0.0), (N, 1)).astype(np.float32),
        "offs": striped(idx),
    }


def reference(xT, w8_words, w8_scales, w4_words, w4_scales, b, gate, offs):
    idx = unstriped(offs)
    w = np.stack([np.concatenate([unpack_weight(w8_words[e], w8_scales[e], "e4m3"), unpack_weight(w4_words[e], w4_scales[e], "e2m1")]) for e in range(E)])
    xq = mxq(np.concatenate([f64(xT), np.zeros((K, E * C - T))], axis=1)[:, idx], 0, "e4m3")
    y = by_expert(w, xq)
    y = y + np.repeat(f64(b), C, axis=1)
    out = np.zeros((N, E * C))
    out[:, idx] = f64(gate) * y
    return out[:, :T]

@@ -1,0 +1,186 @@
+from contextlib import ExitStack
+
+import concourse.mybir as mybir
+
+K, T, E, C, N = 2560, 640, 8, 128, 128
+K8 = 1024
+SLOTS = E * C
+FLOPS = 2 * K * N * SLOTS
+
+F32 = mybir.dt.float32
+BF16 = mybir.dt.bfloat16
+I32 = mybir.dt.int32
+U32 = mybir.dt.uint32
+U16 = mybir.dt.uint16
+U8 = mybir.dt.uint8
+FP8X4 = mybir.dt.float8_e4m3fn_x4
+FP4X4 = mybir.dt.float4_e2m1fn_x4
+COPY = mybir.ActivationFunctionType.Copy
+IDENTITY = mybir.ActivationFunctionType.Identity
+MULT = mybir.AluOpType.mult
+
+P = 128
+PACK = 4
+K_PASS = P * PACK
+PASSES8 = K8 // K_PASS
+PASSES4 = (K - K8) // K_PASS
+LIST_COL = 16
+
+PASS_ORDER = ((2, 0, 0), (3, 1, 0), (0, 1, 4), (1, 1, 8), (4, 1, 12))
+FIRST_CUTS = ((0, 256), (256, 512), (512, 640))
+LATER_CUTS = ((0, 512), (512, 640))
+HALF = SLOTS // 2
+QUARTER = SLOTS // 4
+
+
+def tile_moe_pad_lin_bias_kernel(
+    tc, xT, w8_words, w8_scales, w4_words, w4_scales, b, gate, offs, out
+):
+    nc = tc.nc
+    with ExitStack() as ctx:
+        keep = ctx.enter_context(tc.tile_pool(name="keep", bufs=1))
+        psum = ctx.enter_context(tc.psum_pool(name="psum", bufs=1))
+
+        offsets = keep.tile([P, SLOTS // LIST_COL], U16, name="offsets")
+
+        def slots(j0, j1):
+            return offsets[:, j0 // LIST_COL : j1 // LIST_COL]
+
+        passes = [a for a, tile_no, row in PASS_ORDER]
+        token_words = {a: keep.tile([P, SLOTS], I32, name="token_words%d" % a, align_bytes=64) for a in passes}
+        slot_words = {a: keep.tile([P, SLOTS], U32, name="slot_words%d" % a, align_bytes=64) for a in passes}
+        token_bytes = [keep.tile([P, SLOTS], U8, name="token_bytes%d" % i, align_bytes=64) for i in range(2)]
+        slot_bytes = [keep.tile([P, SLOTS], U8, name="slot_bytes%d" % i, align_bytes=64) for i in range(2)]
+        moved_bytes = keep.tile([P, SLOTS], U8, name="moved_bytes", align_bytes=64)
+        w8 = keep.tile([P, E, PASSES8, PACK * N], U8, name="w8", align_bytes=64)
+        w4 = keep.tile([P, E, PASSES4, 2 * N], U8, name="w4", align_bytes=64)
+        w8_plane = keep.tile([P, E, PASSES8, N], U8, name="w8_plane", align_bytes=64)
+        w4_plane = keep.tile([P, E, PASSES4, N], U8, name="w4_plane", align_bytes=64)
+        bias = keep.tile([P, E], F32, name="bias")
+        gates = keep.tile([P, SLOTS], F32, name="gates")
+        y = keep.tile([P, SLOTS], F32, name="y")
+        window = keep.tile([P, SLOTS], F32, name="window")
+        sums = [psum.tile([P, C], F32, name="sums%d" % e) for e in range(E)]
+
+        raw = {}
+        first = passes[0]
+        for t0, t1 in FIRST_CUTS:
+            piece = keep.tile([P, PACK, t1 - t0], F32, name="raw%d_%d" % (first, t0))
+            rows = xT[first * K_PASS : (first + 1) * K_PASS, t0:t1]
+            nc.sync.dma_start(out=piece[:], in_=rows.rearrange("(p r) t -> p r t", r=PACK))
+            raw[first, t0] = piece[:]
+        nc.sync.dma_start(offsets[:], offs)
+        for a in passes[1:]:
+            whole = keep.tile([P, PACK, T], F32, name="raw%d" % a)
+            rows = xT[a * K_PASS : (a + 1) * K_PASS, :]
+            nc.sync.dma_start(out=whole[:], in_=rows.rearrange("(p r) t -> p r t", r=PACK))
+            for t0, t1 in LATER_CUTS:
+                raw[a, t0] = whole[:, :, t0:t1]
+
+        nc.vector.memset(w4_plane[:].rearrange("p e a n -> p (e a n)").bitcast(I32), 0)
+        nc.vector.memset(w8_plane[:].rearrange("p e a n -> p (e a n)").bitcast(I32), 0)
+        nc.vector.memset(token_bytes[0][:].bitcast(I32), 0)
+        nc.vector.memset(token_words[first][:, T:], 0)
+        nc.vector.memset(token_bytes[1][:].bitcast(I32), 0)
+        for a in passes[1:]:
+            nc.vector.memset(token_words[a][:, T:], 0)
+        nc.vector.memset(moved_bytes[:].bitcast(I32), 0)
+
+        for plane, scales in ((w4_plane, w4_scales), (w8_plane, w8_scales)):
+            by_row = scales.rearrange("e a (g r) n -> r g (e a) n", r=4)
+            for r in range(4):
+                nc.gpsimd.dma_start(
+                    out=plane[r:P:32].rearrange("p e a n -> p (e a) n").bitcast(I32),
+                    in_=by_row[r].bitcast(I32),
+                )
+        nc.sync.dma_start(out=bias[:], in_=b)
+        for e0, e1 in ((0, 2), (2, 4), (4, 8)):
+            nc.sync.dma_start(
+                out=w4[:, e0:e1].rearrange("p e a n -> p (e a) n").bitcast(I32),
+                in_=w4_words[e0:e1].rearrange("e a p n -> p (e a) n").bitcast(I32),
+            )
+            nc.sync.dma_start(
+                out=w8[:, e0:e1].rearrange("p e a n -> p (e a) n").bitcast(I32),
+                in_=w8_words[e0:e1].rearrange("e a p n r -> p (e a) (n r)").bitcast(I32),
+            )
+            if e0 % 4 == 0:
+                nc.sync.dma_start(out=gates[:, e0 * C : e0 * C + HALF], in_=gate[:, e0 * C : e0 * C + HALF])
+
+        def quantise(a, tile_no, row):
+            cuts = FIRST_CUTS if a == first else LATER_CUTS
+            grouped = keep.tile([P, T, PACK], BF16, name="grouped%d" % a, align_bytes=64)
+            for t0, t1 in cuts:
+                dst = grouped[:, t0:t1, :].rearrange("p (c i) r -> p c r i", i=4)
+                src = raw[a, t0].rearrange("p r (c i) -> p c r i", i=4)
+                if a == first and t0 > 0:
+                    nc.vector.tensor_copy(out=dst, in_=src)
+                else:
+                    nc.scalar.activation(out=dst, in_=src, func=COPY)
+            order = cuts[1:] + cuts[:1] if a == first else cuts
+            for t0, t1 in order:
+                nc.vector.quantize_mx(
+                    out=token_words[a][:, t0:t1].bitcast(FP8X4),
+                    scales=token_bytes[tile_no][row:P, t0:t1],
+                    in_=grouped[:, t0:t1, :].rearrange("p t r -> p (t r)"),
+                )
+
+        def gather_words(a, j0, j1):
+            nc.vector.tensor_copy(
+                out=slot_words[a][:, j0:j1], in_=token_words[a][:].bitcast(U32).indirect(slots(j0, j1))
+            )
+
+        def gather_bytes(tile_no):
+            for j0 in range(0, SLOTS, HALF):
+                nc.vector.tensor_copy(
+                    out=slot_bytes[tile_no][:, j0 : j0 + HALF],
+                    in_=token_bytes[tile_no][:].indirect(slots(j0, j0 + HALF)),
+                )
+
+        def multiply(e, a, plane, start, stop):
+            cols = slice(e * C, (e + 1) * C)
+            if a < PASSES8:
+                codes, scales = w8[:, e, a, :].bitcast(FP8X4), w8_plane[:, e, a, :]
+            else:
+                codes, scales = w4[:, e, a - PASSES8, :].bitcast(FP4X4), w4_plane[:, e, a - PASSES8, :]
+            nc.tensor.matmul_mx(
+                out=sums[e][:],
+                lhsT=codes,
+                lhsT_scale=scales,
+                rhs=slot_words[a][:, cols].bitcast(FP8X4),
+                rhs_scale=plane[:, cols],
+                start=start,
+                stop=stop,
+            )
+
+        last, last_tile, last_row = PASS_ORDER[-1]
+        for a, tile_no, row in PASS_ORDER[:-1]:
+            quantise(a, tile_no, row)
+            for j0 in range(0, SLOTS, HALF):
+                gather_words(a, j0, j0 + HALF)
+            if a == first:
+                gather_bytes(tile_no)
+        quantise(last, last_tile, last_row)
+        gather_bytes(last_tile)
+        for j0, queue in ((0, nc.scalar), (HALF, nc.sync)):
+            for r in range(4):
+                queue.dma_start(
+                    out=moved_bytes[r:P:32, j0 : j0 + HALF].bitcast(I32),
+                    in_=slot_bytes[last_tile][last_row + r : P : 32, j0 : j0 + HALF].bitcast(I32),
+                )
+        for j0 in range(0, SLOTS, QUARTER):
+            gather_words(last, j0, j0 + QUARTER)
+
+        sum_order = PASS_ORDER[1:-1] + PASS_ORDER[:1]
+        for j0 in range(0, SLOTS, QUARTER):
+            for e in range(j0 // C, (j0 + QUARTER) // C):
+                for a, tile_no, row in sum_order:
+                    multiply(e, a, slot_bytes[tile_no][row:P], a == sum_order[0][0], False)
+                multiply(e, last, moved_bytes[:], False, True)
+                nc.scalar.activation(
+                    out=y[:, e * C : (e + 1) * C], in_=sums[e][:], func=IDENTITY, bias=bias[:, e : e + 1]
+                )
+            cols = slice(j0, j0 + QUARTER)
+            nc.vector.tensor_tensor(
+                window[:].indirect(slots(j0, j0 + QUARTER)), y[:, cols], gates[:, cols], MULT
+            )
+        nc.sync.dma_start(out=out, in_=window[:, :T])

@@ -27,8 +27,8 @@ PASSES4 = (K - K8) // K_PASS
 LIST_COL = 16
 
 PASS_ORDER = ((2, 0, 0), (3, 1, 0), (0, 1, 4), (1, 1, 8), (4, 1, 12))
-FIRST_CUTS = ((0, 256), (256, 512), (512, 640))
-LATER_CUTS = ((0, 512), (512, 640))
+TOKEN_CUTS = ((0, 256), (256, 512), (512, 640))
+EXPERT_CUTS = ((0, 2), (2, 4), (4, 8))
 HALF = SLOTS // 2
 QUARTER = SLOTS // 4
 
@@ -39,6 +39,7 @@ def tile_moe_pad_lin_bias_kernel(
     nc = tc.nc
     with ExitStack() as ctx:
         keep = ctx.enter_context(tc.tile_pool(name="keep", bufs=1))
+        stream = ctx.enter_context(tc.tile_pool(name="stream", bufs=len(PASS_ORDER) * len(TOKEN_CUTS)))
         psum = ctx.enter_context(tc.psum_pool(name="psum", bufs=1))
 
         offsets = keep.tile([P, SLOTS // LIST_COL], U16, name="offsets")
@@ -52,30 +53,23 @@ def tile_moe_pad_lin_bias_kernel(
         token_bytes = [keep.tile([P, SLOTS], U8, name="token_bytes%d" % i, align_bytes=64) for i in range(2)]
         slot_bytes = [keep.tile([P, SLOTS], U8, name="slot_bytes%d" % i, align_bytes=64) for i in range(2)]
         moved_bytes = keep.tile([P, SLOTS], U8, name="moved_bytes", align_bytes=64)
-        w8 = keep.tile([P, E, PASSES8, PACK * N], U8, name="w8", align_bytes=64)
-        w4 = keep.tile([P, E, PASSES4, 2 * N], U8, name="w4", align_bytes=64)
         w8_plane = keep.tile([P, E, PASSES8, N], U8, name="w8_plane", align_bytes=64)
         w4_plane = keep.tile([P, E, PASSES4, N], U8, name="w4_plane", align_bytes=64)
         bias = keep.tile([P, E], F32, name="bias")
-        gates = keep.tile([P, SLOTS], F32, name="gates")
         y = keep.tile([P, SLOTS], F32, name="y")
         window = keep.tile([P, SLOTS], F32, name="window")
         sums = [psum.tile([P, C], F32, name="sums%d" % e) for e in range(E)]
 
         raw = {}
         first = passes[0]
-        for t0, t1 in FIRST_CUTS:
-            piece = keep.tile([P, PACK, t1 - t0], F32, name="raw%d_%d" % (first, t0))
-            rows = xT[first * K_PASS : (first + 1) * K_PASS, t0:t1]
-            nc.sync.dma_start(out=piece[:], in_=rows.rearrange("(p r) t -> p r t", r=PACK))
-            raw[first, t0] = piece[:]
-        nc.sync.dma_start(offsets[:], offs)
-        for a in passes[1:]:
-            whole = keep.tile([P, PACK, T], F32, name="raw%d" % a)
-            rows = xT[a * K_PASS : (a + 1) * K_PASS, :]
-            nc.sync.dma_start(out=whole[:], in_=rows.rearrange("(p r) t -> p r t", r=PACK))
-            for t0, t1 in LATER_CUTS:
-                raw[a, t0] = whole[:, :, t0:t1]
+        for a in passes:
+            for t0, t1 in TOKEN_CUTS:
+                piece = stream.tile([P, PACK, t1 - t0], F32, name="raw%d_%d" % (a, t0), tag="stream", align_bytes=64)
+                rows = xT[a * K_PASS : (a + 1) * K_PASS, t0:t1]
+                nc.sync.dma_start(out=piece[:], in_=rows.rearrange("(p r) t -> p r t", r=PACK))
+                raw[a, t0] = piece
+            if a == first:
+                nc.sync.dma_start(offsets[:], offs)
 
         nc.vector.memset(w4_plane[:].rearrange("p e a n -> p (e a n)").bitcast(I32), 0)
         nc.vector.memset(w8_plane[:].rearrange("p e a n -> p (e a n)").bitcast(I32), 0)
@@ -89,35 +83,37 @@ def tile_moe_pad_lin_bias_kernel(
         for plane, scales in ((w4_plane, w4_scales), (w8_plane, w8_scales)):
             by_row = scales.rearrange("e a (g r) n -> r g (e a) n", r=4)
             for r in range(4):
-                nc.gpsimd.dma_start(
+                nc.sync.dma_start(
                     out=plane[r:P:32].rearrange("p e a n -> p (e a) n").bitcast(I32),
                     in_=by_row[r].bitcast(I32),
                 )
         nc.sync.dma_start(out=bias[:], in_=b)
-        for e0, e1 in ((0, 2), (2, 4), (4, 8)):
+        w4, w8, gates = {}, {}, {}
+        for e0, e1 in EXPERT_CUTS:
+            codes4 = stream.tile([P, e1 - e0, PASSES4, 2 * N], U8, name="w4_%d" % e0, tag="stream", align_bytes=64)
             nc.sync.dma_start(
-                out=w4[:, e0:e1].rearrange("p e a n -> p (e a) n").bitcast(I32),
+                out=codes4[:].rearrange("p e a n -> p (e a) n").bitcast(I32),
                 in_=w4_words[e0:e1].rearrange("e a p n -> p (e a) n").bitcast(I32),
             )
+            codes8 = stream.tile([P, e1 - e0, PASSES8, PACK * N], U8, name="w8_%d" % e0, tag="stream", align_bytes=64)
             nc.sync.dma_start(
-                out=w8[:, e0:e1].rearrange("p e a n -> p (e a) n").bitcast(I32),
+                out=codes8[:].rearrange("p e a n -> p (e a) n").bitcast(I32),
                 in_=w8_words[e0:e1].rearrange("e a p n r -> p (e a) (n r)").bitcast(I32),
             )
-            if e0 % 4 == 0:
-                nc.sync.dma_start(out=gates[:, e0 * C : e0 * C + HALF], in_=gate[:, e0 * C : e0 * C + HALF])
+            gates[e0] = stream.tile([P, (e1 - e0) * C], F32, name="gates%d" % e0, tag="stream", align_bytes=64)
+            nc.sync.dma_start(out=gates[e0][:], in_=gate[:, e0 * C : e1 * C])
+            for e in range(e0, e1):
+                w4[e], w8[e] = codes4[:, e - e0], codes8[:, e - e0]
 
         def quantise(a, tile_no, row):
-            cuts = FIRST_CUTS if a == first else LATER_CUTS
             grouped = keep.tile([P, T, PACK], BF16, name="grouped%d" % a, align_bytes=64)
-            for t0, t1 in cuts:
+            for t0, t1 in TOKEN_CUTS:
                 dst = grouped[:, t0:t1, :].rearrange("p (c i) r -> p c r i", i=4)
-                src = raw[a, t0].rearrange("p r (c i) -> p c r i", i=4)
+                src = raw[a, t0][:].rearrange("p r (c i) -> p c r i", i=4)
                 if a == first and t0 > 0:
                     nc.vector.tensor_copy(out=dst, in_=src)
                 else:
                     nc.scalar.activation(out=dst, in_=src, func=COPY)
-            order = cuts[1:] + cuts[:1] if a == first else cuts
-            for t0, t1 in order:
                 nc.vector.quantize_mx(
                     out=token_words[a][:, t0:t1].bitcast(FP8X4),
                     scales=token_bytes[tile_no][row:P, t0:t1],
@@ -129,19 +125,17 @@ def tile_moe_pad_lin_bias_kernel(
                 out=slot_words[a][:, j0:j1], in_=token_words[a][:].bitcast(U32).indirect(slots(j0, j1))
             )
 
-        def gather_bytes(tile_no):
-            for j0 in range(0, SLOTS, HALF):
-                nc.vector.tensor_copy(
-                    out=slot_bytes[tile_no][:, j0 : j0 + HALF],
-                    in_=token_bytes[tile_no][:].indirect(slots(j0, j0 + HALF)),
-                )
+        def gather_bytes(tile_no, j0, j1):
+            nc.vector.tensor_copy(
+                out=slot_bytes[tile_no][:, j0:j1], in_=token_bytes[tile_no][:].indirect(slots(j0, j1))
+            )
 
         def multiply(e, a, plane, start, stop):
             cols = slice(e * C, (e + 1) * C)
             if a < PASSES8:
-                codes, scales = w8[:, e, a, :].bitcast(FP8X4), w8_plane[:, e, a, :]
+                codes, scales = w8[e][:, a, :].bitcast(FP8X4), w8_plane[:, e, a, :]
             else:
-                codes, scales = w4[:, e, a - PASSES8, :].bitcast(FP4X4), w4_plane[:, e, a - PASSES8, :]
+                codes, scales = w4[e][:, a - PASSES8, :].bitcast(FP4X4), w4_plane[:, e, a - PASSES8, :]
             nc.tensor.matmul_mx(
                 out=sums[e][:],
                 lhsT=codes,
@@ -153,14 +147,18 @@ def tile_moe_pad_lin_bias_kernel(
             )
 
         last, last_tile, last_row = PASS_ORDER[-1]
-        for a, tile_no, row in PASS_ORDER[:-1]:
-            quantise(a, tile_no, row)
-            for j0 in range(0, SLOTS, HALF):
-                gather_words(a, j0, j0 + HALF)
-            if a == first:
-                gather_bytes(tile_no)
-        quantise(last, last_tile, last_row)
-        gather_bytes(last_tile)
+        quantise(*PASS_ORDER[0])
+        gather_words(first, 0, HALF)
+        gather_words(first, HALF, SLOTS)
+        gather_bytes(0, 0, HALF)
+        quantise(*PASS_ORDER[1])
+        gather_bytes(0, HALF, SLOTS)
+        for i in range(1, len(PASS_ORDER) - 1):
+            gather_words(passes[i], 0, HALF)
+            quantise(*PASS_ORDER[i + 1])
+            gather_words(passes[i], HALF, SLOTS)
+        gather_bytes(last_tile, 0, HALF)
+        gather_bytes(last_tile, HALF, SLOTS)
         for j0, queue in ((0, nc.scalar), (HALF, nc.sync)):
             for r in range(4):
                 queue.dma_start(
@@ -171,16 +169,14 @@ def tile_moe_pad_lin_bias_kernel(
             gather_words(last, j0, j0 + QUARTER)
 
         sum_order = PASS_ORDER[1:-1] + PASS_ORDER[:1]
-        for j0 in range(0, SLOTS, QUARTER):
-            for e in range(j0 // C, (j0 + QUARTER) // C):
+        for e0, e1 in EXPERT_CUTS:
+            for e in range(e0, e1):
                 for a, tile_no, row in sum_order:
                     multiply(e, a, slot_bytes[tile_no][row:P], a == sum_order[0][0], False)
                 multiply(e, last, moved_bytes[:], False, True)
                 nc.scalar.activation(
                     out=y[:, e * C : (e + 1) * C], in_=sums[e][:], func=IDENTITY, bias=bias[:, e : e + 1]
                 )
-            cols = slice(j0, j0 + QUARTER)
-            nc.vector.tensor_tensor(
-                window[:].indirect(slots(j0, j0 + QUARTER)), y[:, cols], gates[:, cols], MULT
-            )
+            j0, j1 = e0 * C, e1 * C
+            nc.vector.tensor_tensor(window[:].indirect(slots(j0, j1)), y[:, j0:j1], gates[e0][:], MULT)
         nc.sync.dma_start(out=out, in_=window[:, :T])

@@ -28,7 +28,9 @@ LIST_COL = 16
 
 PASS_ORDER = ((2, 0, 0), (3, 1, 0), (0, 1, 4), (1, 1, 8), (4, 1, 12))
 TOKEN_CUTS = ((0, 256), (256, 512), (512, 640))
-EXPERT_CUTS = ((0, 2), (2, 4), (4, 8))
+HALF_TOKENS = ((0, 320), (320, 640))
+EXPERT_CUTS = ((0, 2), (2, 6), (6, 8))
+MOVE_ROWS = ((0, 64), (64, 96), (96, 112))
 HALF = SLOTS // 2
 QUARTER = SLOTS // 4
 
@@ -39,7 +41,7 @@ def tile_moe_pad_lin_bias_kernel(
     nc = tc.nc
     with ExitStack() as ctx:
         keep = ctx.enter_context(tc.tile_pool(name="keep", bufs=1))
-        stream = ctx.enter_context(tc.tile_pool(name="stream", bufs=len(PASS_ORDER) * len(TOKEN_CUTS)))
+        stream = ctx.enter_context(tc.tile_pool(name="stream", bufs=len(TOKEN_CUTS) + (len(PASS_ORDER) - 1) * len(HALF_TOKENS)))
         psum = ctx.enter_context(tc.psum_pool(name="psum", bufs=1))
 
         offsets = keep.tile([P, SLOTS // LIST_COL], U16, name="offsets")
@@ -48,13 +50,15 @@ def tile_moe_pad_lin_bias_kernel(
             return offsets[:, j0 // LIST_COL : j1 // LIST_COL]
 
         passes = [a for a, tile_no, row in PASS_ORDER]
-        token_words = {a: keep.tile([P, SLOTS], I32, name="token_words%d" % a, align_bytes=64) for a in passes}
+        word_tiles = [keep.tile([P, SLOTS], I32, name="token_words%d" % i, align_bytes=64) for i in range(2)]
+        token_words = {a: word_tiles[i % 2] for i, a in enumerate(passes)}
         slot_words = {a: keep.tile([P, SLOTS], U32, name="slot_words%d" % a, align_bytes=64) for a in passes}
-        token_bytes = [keep.tile([P, SLOTS], U8, name="token_bytes%d" % i, align_bytes=64) for i in range(2)]
+        token_bytes = [keep.tile([P, SLOTS + 4], U8, name="token_bytes%d" % i, align_bytes=64) for i in range(2)]
         slot_bytes = [keep.tile([P, SLOTS], U8, name="slot_bytes%d" % i, align_bytes=64) for i in range(2)]
-        moved_bytes = keep.tile([P, SLOTS], U8, name="moved_bytes", align_bytes=64)
+        moved_bytes = keep.tile([P, SLOTS + 4], U8, name="moved_bytes", align_bytes=64)
         w8_plane = keep.tile([P, E, PASSES8, N], U8, name="w8_plane", align_bytes=64)
-        w4_plane = keep.tile([P, E, PASSES4, N], U8, name="w4_plane", align_bytes=64)
+        w4_padded = keep.tile([P, E * PASSES4 * N + 4], U8, name="w4_plane", align_bytes=64)
+        w4_plane = w4_padded[:, : E * PASSES4 * N].rearrange("p (e a n) -> p e a n", e=E, a=PASSES4)
         bias = keep.tile([P, E], F32, name="bias")
         y = keep.tile([P, SLOTS], F32, name="y")
         window = keep.tile([P, SLOTS], F32, name="window")
@@ -63,31 +67,29 @@ def tile_moe_pad_lin_bias_kernel(
         raw = {}
         first = passes[0]
         for a in passes:
-            for t0, t1 in TOKEN_CUTS:
+            for t0, t1 in TOKEN_CUTS if a == first else HALF_TOKENS:
                 piece = stream.tile([P, PACK, t1 - t0], F32, name="raw%d_%d" % (a, t0), tag="stream", align_bytes=64)
                 rows = xT[a * K_PASS : (a + 1) * K_PASS, t0:t1]
                 nc.sync.dma_start(out=piece[:], in_=rows.rearrange("(p r) t -> p r t", r=PACK))
                 raw[a, t0] = piece
             if a == first:
                 nc.sync.dma_start(offsets[:], offs)
+                nc.sync.dma_start(out=bias[:], in_=b)
 
-        nc.vector.memset(w4_plane[:].rearrange("p e a n -> p (e a n)").bitcast(I32), 0)
-        nc.vector.memset(w8_plane[:].rearrange("p e a n -> p (e a n)").bitcast(I32), 0)
-        nc.vector.memset(token_bytes[0][:].bitcast(I32), 0)
-        nc.vector.memset(token_words[first][:, T:], 0)
-        nc.vector.memset(token_bytes[1][:].bitcast(I32), 0)
-        for a in passes[1:]:
-            nc.vector.memset(token_words[a][:, T:], 0)
+        nc.gpsimd.memset(w8_plane[:].rearrange("p e a n -> p (e a n)").bitcast(I32), 0)
+        nc.vector.memset(w4_padded[:].bitcast(I32), 0)
+        for i in range(2):
+            nc.vector.memset(token_bytes[i][:].bitcast(I32), 0)
+            nc.vector.memset(word_tiles[i][:, T - 1 :], 0)
         nc.vector.memset(moved_bytes[:].bitcast(I32), 0)
 
-        for plane, scales in ((w4_plane, w4_scales), (w8_plane, w8_scales)):
+        for plane, scales, queue in ((w8_plane, w8_scales, nc.gpsimd), (w4_plane, w4_scales, nc.sync)):
             by_row = scales.rearrange("e a (g r) n -> r g (e a) n", r=4)
             for r in range(4):
-                nc.sync.dma_start(
+                queue.dma_start(
                     out=plane[r:P:32].rearrange("p e a n -> p (e a) n").bitcast(I32),
                     in_=by_row[r].bitcast(I32),
                 )
-        nc.sync.dma_start(out=bias[:], in_=b)
         w4, w8, gates = {}, {}, {}
         for e0, e1 in EXPERT_CUTS:
             codes4 = stream.tile([P, e1 - e0, PASSES4, 2 * N], U8, name="w4_%d" % e0, tag="stream", align_bytes=64)
@@ -100,20 +102,23 @@ def tile_moe_pad_lin_bias_kernel(
                 out=codes8[:].rearrange("p e a n -> p (e a) n").bitcast(I32),
                 in_=w8_words[e0:e1].rearrange("e a p n r -> p (e a) (n r)").bitcast(I32),
             )
-            gates[e0] = stream.tile([P, (e1 - e0) * C], F32, name="gates%d" % e0, tag="stream", align_bytes=64)
-            nc.sync.dma_start(out=gates[e0][:], in_=gate[:, e0 * C : e1 * C])
+            if e0 < E // 2:
+                j0 = HALF * len(gates)
+                gates[j0] = stream.tile([P, HALF], F32, name="gates%d" % j0, tag="stream", align_bytes=64)
+                nc.sync.dma_start(out=gates[j0][:], in_=gate[:, j0 : j0 + HALF])
             for e in range(e0, e1):
                 w4[e], w8[e] = codes4[:, e - e0], codes8[:, e - e0]
 
         def quantise(a, tile_no, row):
             grouped = keep.tile([P, T, PACK], BF16, name="grouped%d" % a, align_bytes=64)
-            for t0, t1 in TOKEN_CUTS:
+            for t0, t1 in TOKEN_CUTS if a == first else HALF_TOKENS:
                 dst = grouped[:, t0:t1, :].rearrange("p (c i) r -> p c r i", i=4)
                 src = raw[a, t0][:].rearrange("p r (c i) -> p c r i", i=4)
                 if a == first and t0 > 0:
                     nc.vector.tensor_copy(out=dst, in_=src)
                 else:
                     nc.scalar.activation(out=dst, in_=src, func=COPY)
+            for t0, t1 in TOKEN_CUTS:
                 nc.vector.quantize_mx(
                     out=token_words[a][:, t0:t1].bitcast(FP8X4),
                     scales=token_bytes[tile_no][row:P, t0:t1],
@@ -127,7 +132,7 @@ def tile_moe_pad_lin_bias_kernel(
 
         def gather_bytes(tile_no, j0, j1):
             nc.vector.tensor_copy(
-                out=slot_bytes[tile_no][:, j0:j1], in_=token_bytes[tile_no][:].indirect(slots(j0, j1))
+                out=slot_bytes[tile_no][:, j0:j1], in_=token_bytes[tile_no][:, :SLOTS].indirect(slots(j0, j1))
             )
 
         def multiply(e, a, plane, start, stop):
@@ -153,30 +158,34 @@ def tile_moe_pad_lin_bias_kernel(
         gather_bytes(0, 0, HALF)
         quantise(*PASS_ORDER[1])
         gather_bytes(0, HALF, SLOTS)
-        for i in range(1, len(PASS_ORDER) - 1):
+        for i in range(1, len(PASS_ORDER) - 2):
             gather_words(passes[i], 0, HALF)
             quantise(*PASS_ORDER[i + 1])
             gather_words(passes[i], HALF, SLOTS)
+        gather_words(passes[-2], 0, HALF)
+        quantise(*PASS_ORDER[-1])
+        gather_words(passes[-2], HALF, HALF + QUARTER)
         gather_bytes(last_tile, 0, HALF)
         gather_bytes(last_tile, HALF, SLOTS)
-        for j0, queue in ((0, nc.scalar), (HALF, nc.sync)):
-            for r in range(4):
-                queue.dma_start(
-                    out=moved_bytes[r:P:32, j0 : j0 + HALF].bitcast(I32),
-                    in_=slot_bytes[last_tile][last_row + r : P : 32, j0 : j0 + HALF].bitcast(I32),
-                )
+        for r0, r1 in MOVE_ROWS:
+            nc.scalar.dma_start(
+                out=moved_bytes[r0:r1, :SLOTS].bitcast(I32),
+                in_=slot_bytes[last_tile][last_row + r0 : last_row + r1, :].bitcast(I32),
+            )
+        gather_words(passes[-2], HALF + QUARTER, SLOTS)
         for j0 in range(0, SLOTS, QUARTER):
             gather_words(last, j0, j0 + QUARTER)
 
         sum_order = PASS_ORDER[1:-1] + PASS_ORDER[:1]
-        for e0, e1 in EXPERT_CUTS:
-            for e in range(e0, e1):
+        for j0 in range(0, SLOTS, QUARTER):
+            j1 = j0 + QUARTER
+            for e in range(j0 // C, j1 // C):
                 for a, tile_no, row in sum_order:
                     multiply(e, a, slot_bytes[tile_no][row:P], a == sum_order[0][0], False)
                 multiply(e, last, moved_bytes[:], False, True)
                 nc.scalar.activation(
                     out=y[:, e * C : (e + 1) * C], in_=sums[e][:], func=IDENTITY, bias=bias[:, e : e + 1]
                 )
-            j0, j1 = e0 * C, e1 * C
-            nc.vector.tensor_tensor(window[:].indirect(slots(j0, j1)), y[:, j0:j1], gates[e0][:], MULT)
+            gate_cols = gates[j0 - j0 % HALF][:, j0 % HALF : j0 % HALF + QUARTER]
+            nc.vector.tensor_tensor(window[:].indirect(slots(j0, j1)), y[:, j0:j1], gate_cols, MULT)
         nc.sync.dma_start(out=out, in_=window[:, :T])

from contextlib import ExitStack

import concourse.mybir as mybir

K, T, E, C, N = 2560, 640, 8, 128, 128
K8 = 1024
SLOTS = E * C
FLOPS = 2 * K * N * SLOTS

F32 = mybir.dt.float32
BF16 = mybir.dt.bfloat16
I32 = mybir.dt.int32
U32 = mybir.dt.uint32
U16 = mybir.dt.uint16
U8 = mybir.dt.uint8
FP8X4 = mybir.dt.float8_e4m3fn_x4
FP4X4 = mybir.dt.float4_e2m1fn_x4
COPY = mybir.ActivationFunctionType.Copy
IDENTITY = mybir.ActivationFunctionType.Identity
MULT = mybir.AluOpType.mult

P = 128
PACK = 4
K_PASS = P * PACK
PASSES8 = K8 // K_PASS
PASSES4 = (K - K8) // K_PASS
LIST_COL = 16

PASS_ORDER = ((2, 0, 0), (3, 1, 0), (0, 1, 4), (1, 1, 8), (4, 1, 12))
TOKEN_CUTS = ((0, 256), (256, 512), (512, 640))
HALF_TOKENS = ((0, 320), (320, 640))
EXPERT_CUTS = ((0, 2), (2, 6), (6, 8))
MOVE_ROWS = ((0, 64), (64, 96), (96, 112))
HALF = SLOTS // 2
QUARTER = SLOTS // 4


def tile_moe_pad_lin_bias_kernel(
    tc, xT, w8_words, w8_scales, w4_words, w4_scales, b, gate, offs, out
):
    nc = tc.nc
    with ExitStack() as ctx:
        keep = ctx.enter_context(tc.tile_pool(name="keep", bufs=1))
        stream = ctx.enter_context(tc.tile_pool(name="stream", bufs=len(TOKEN_CUTS) + (len(PASS_ORDER) - 1) * len(HALF_TOKENS)))
        psum = ctx.enter_context(tc.psum_pool(name="psum", bufs=1))

        offsets = keep.tile([P, SLOTS // LIST_COL], U16, name="offsets")

        def slots(j0, j1):
            return offsets[:, j0 // LIST_COL : j1 // LIST_COL]

        passes = [a for a, tile_no, row in PASS_ORDER]
        word_tiles = [keep.tile([P, SLOTS], I32, name="token_words%d" % i, align_bytes=64) for i in range(2)]
        token_words = {a: word_tiles[i % 2] for i, a in enumerate(passes)}
        slot_words = {a: keep.tile([P, SLOTS], U32, name="slot_words%d" % a, align_bytes=64) for a in passes}
        token_bytes = [keep.tile([P, SLOTS + 4], U8, name="token_bytes%d" % i, align_bytes=64) for i in range(2)]
        slot_bytes = [keep.tile([P, SLOTS], U8, name="slot_bytes%d" % i, align_bytes=64) for i in range(2)]
        moved_bytes = keep.tile([P, SLOTS + 4], U8, name="moved_bytes", align_bytes=64)
        w8_plane = keep.tile([P, E, PASSES8, N], U8, name="w8_plane", align_bytes=64)
        w4_padded = keep.tile([P, E * PASSES4 * N + 4], U8, name="w4_plane", align_bytes=64)
        w4_plane = w4_padded[:, : E * PASSES4 * N].rearrange("p (e a n) -> p e a n", e=E, a=PASSES4)
        bias = keep.tile([P, E], F32, name="bias")
        y = keep.tile([P, SLOTS], F32, name="y")
        window = keep.tile([P, SLOTS], F32, name="window")
        sums = [psum.tile([P, C], F32, name="sums%d" % e) for e in range(E)]

        raw = {}
        first = passes[0]
        for a in passes:
            for t0, t1 in TOKEN_CUTS if a == first else HALF_TOKENS:
                piece = stream.tile([P, PACK, t1 - t0], F32, name="raw%d_%d" % (a, t0), tag="stream", align_bytes=64)
                rows = xT[a * K_PASS : (a + 1) * K_PASS, t0:t1]
                nc.sync.dma_start(out=piece[:], in_=rows.rearrange("(p r) t -> p r t", r=PACK))
                raw[a, t0] = piece
            if a == first:
                nc.sync.dma_start(offsets[:], offs)
                nc.sync.dma_start(out=bias[:], in_=b)

        nc.gpsimd.memset(w8_plane[:].rearrange("p e a n -> p (e a n)").bitcast(I32), 0)
        nc.vector.memset(w4_padded[:].bitcast(I32), 0)
        for i in range(2):
            nc.vector.memset(token_bytes[i][:].bitcast(I32), 0)
            nc.vector.memset(word_tiles[i][:, T - 1 :], 0)
        nc.vector.memset(moved_bytes[:].bitcast(I32), 0)

        for plane, scales, queue in ((w8_plane, w8_scales, nc.gpsimd), (w4_plane, w4_scales, nc.sync)):
            by_row = scales.rearrange("e a (g r) n -> r g (e a) n", r=4)
            for r in range(4):
                queue.dma_start(
                    out=plane[r:P:32].rearrange("p e a n -> p (e a) n").bitcast(I32),
                    in_=by_row[r].bitcast(I32),
                )
        w4, w8, gates = {}, {}, {}
        for e0, e1 in EXPERT_CUTS:
            codes4 = stream.tile([P, e1 - e0, PASSES4, 2 * N], U8, name="w4_%d" % e0, tag="stream", align_bytes=64)
            nc.sync.dma_start(
                out=codes4[:].rearrange("p e a n -> p (e a) n").bitcast(I32),
                in_=w4_words[e0:e1].rearrange("e a p n -> p (e a) n").bitcast(I32),
            )
            codes8 = stream.tile([P, e1 - e0, PASSES8, PACK * N], U8, name="w8_%d" % e0, tag="stream", align_bytes=64)
            nc.sync.dma_start(
                out=codes8[:].rearrange("p e a n -> p (e a) n").bitcast(I32),
                in_=w8_words[e0:e1].rearrange("e a p n r -> p (e a) (n r)").bitcast(I32),
            )
            if e0 < E // 2:
                j0 = HALF * len(gates)
                gates[j0] = stream.tile([P, HALF], F32, name="gates%d" % j0, tag="stream", align_bytes=64)
                nc.sync.dma_start(out=gates[j0][:], in_=gate[:, j0 : j0 + HALF])
            for e in range(e0, e1):
                w4[e], w8[e] = codes4[:, e - e0], codes8[:, e - e0]

        def quantise(a, tile_no, row):
            grouped = keep.tile([P, T, PACK], BF16, name="grouped%d" % a, align_bytes=64)
            for t0, t1 in TOKEN_CUTS if a == first else HALF_TOKENS:
                dst = grouped[:, t0:t1, :].rearrange("p (c i) r -> p c r i", i=4)
                src = raw[a, t0][:].rearrange("p r (c i) -> p c r i", i=4)
                if a == first and t0 > 0:
                    nc.vector.tensor_copy(out=dst, in_=src)
                else:
                    nc.scalar.activation(out=dst, in_=src, func=COPY)
            for t0, t1 in TOKEN_CUTS:
                nc.vector.quantize_mx(
                    out=token_words[a][:, t0:t1].bitcast(FP8X4),
                    scales=token_bytes[tile_no][row:P, t0:t1],
                    in_=grouped[:, t0:t1, :].rearrange("p t r -> p (t r)"),
                )

        def gather_words(a, j0, j1):
            nc.vector.tensor_copy(
                out=slot_words[a][:, j0:j1], in_=token_words[a][:].bitcast(U32).indirect(slots(j0, j1))
            )

        def gather_bytes(tile_no, j0, j1):
            nc.vector.tensor_copy(
                out=slot_bytes[tile_no][:, j0:j1], in_=token_bytes[tile_no][:, :SLOTS].indirect(slots(j0, j1))
            )

        def multiply(e, a, plane, start, stop):
            cols = slice(e * C, (e + 1) * C)
            if a < PASSES8:
                codes, scales = w8[e][:, a, :].bitcast(FP8X4), w8_plane[:, e, a, :]
            else:
                codes, scales = w4[e][:, a - PASSES8, :].bitcast(FP4X4), w4_plane[:, e, a - PASSES8, :]
            nc.tensor.matmul_mx(
                out=sums[e][:],
                lhsT=codes,
                lhsT_scale=scales,
                rhs=slot_words[a][:, cols].bitcast(FP8X4),
                rhs_scale=plane[:, cols],
                start=start,
                stop=stop,
            )

        last, last_tile, last_row = PASS_ORDER[-1]
        quantise(*PASS_ORDER[0])
        gather_words(first, 0, HALF)
        gather_words(first, HALF, SLOTS)
        gather_bytes(0, 0, HALF)
        quantise(*PASS_ORDER[1])
        gather_bytes(0, HALF, SLOTS)
        for i in range(1, len(PASS_ORDER) - 2):
            gather_words(passes[i], 0, HALF)
            quantise(*PASS_ORDER[i + 1])
            gather_words(passes[i], HALF, SLOTS)
        gather_words(passes[-2], 0, HALF)
        quantise(*PASS_ORDER[-1])
        gather_words(passes[-2], HALF, HALF + QUARTER)
        gather_bytes(last_tile, 0, HALF)
        gather_bytes(last_tile, HALF, SLOTS)
        for r0, r1 in MOVE_ROWS:
            nc.scalar.dma_start(
                out=moved_bytes[r0:r1, :SLOTS].bitcast(I32),
                in_=slot_bytes[last_tile][last_row + r0 : last_row + r1, :].bitcast(I32),
            )
        gather_words(passes[-2], HALF + QUARTER, SLOTS)
        for j0 in range(0, SLOTS, QUARTER):
            gather_words(last, j0, j0 + QUARTER)

        sum_order = PASS_ORDER[1:-1] + PASS_ORDER[:1]
        for j0 in range(0, SLOTS, QUARTER):
            j1 = j0 + QUARTER
            for e in range(j0 // C, j1 // C):
                for a, tile_no, row in sum_order:
                    multiply(e, a, slot_bytes[tile_no][row:P], a == sum_order[0][0], False)
                multiply(e, last, moved_bytes[:], False, True)
                nc.scalar.activation(
                    out=y[:, e * C : (e + 1) * C], in_=sums[e][:], func=IDENTITY, bias=bias[:, e : e + 1]
                )
            gate_cols = gates[j0 - j0 % HALF][:, j0 % HALF : j0 % HALF + QUARTER]
            nc.vector.tensor_tensor(window[:].indirect(slots(j0, j1)), y[:, j0:j1], gate_cols, MULT)
        nc.sync.dma_start(out=out, in_=window[:, :T])
